import numpy as np, ml_dtypes
CORES = [12,28,60,100,156,228]
N = 6
KT, C = 1, 128
def setup_inputs(rng):
    return {"x": rng.standard_normal((N, 128, KT * C), dtype=np.float32).astype(ml_dtypes.bfloat16)}
def setup_inputs_big(rng):
    d = setup_inputs(rng)
    for k in ("x",): d[k] = (d[k].astype(np.float32) * 1024.0).astype(d[k].dtype)
    return d
def setup_inputs_small(rng):
    d = setup_inputs(rng)
    for k in ("x",): d[k] = (d[k].astype(np.float32) * (1 / 1024.0)).astype(d[k].dtype)
    return d
def setup_inputs_apart(rng):
    d = setup_inputs(rng)
    f = (10.0 ** rng.permutation(np.linspace(-1.5, 1.5, N))).astype(np.float32).reshape(N, 1, 1)
    for k in ("x",): d[k] = (d[k].astype(np.float32) * f).astype(d[k].dtype)
    return d
def reference(x):
    X = x.astype(np.float64)
    y = np.full((N, C, N * C), np.nan)
    for r in range(N):
        for i in range(N):
            s = i
            if s != r: y[r][:, C * i:C * i + C] = sum(X[r][:, C * t:C * t + C].T @ X[s][:, C * t:C * t + C] for t in range(KT))
    return {"y": y.astype(ml_dtypes.bfloat16 if x.dtype != np.float64 else np.float64)}

from concourse.bass import DstId, RemoteDMATransfer

N = 6
C = 128
K_HAND = 8
K_PASS = 8
K_STRAIGHT = 8

SCRATCH = {
    "land": ("sbuf", [128, N * C], "bfloat16"),
    "ysb": ("sbuf", [128, N * C], "bfloat16"),
    "xd": ("dram", [128, C], "bfloat16"),
    "rl": ("dram", [128, C], "bfloat16"),
}
SCRATCH.update({"ps%d" % s: ("psum", [128, 512], "float32") for s in range(N)})

SEMAPHORES = (["ldd", "ldx", "hand", "sent"] + ["a%d" % s for s in range(N)] + ["m%d" % s for s in range(N)]
              + ["cp%d" % i for i in range(3)] + ["st%d" % i for i in range(3)])

_CACHE = {}


def _count(mask):
    return bin(mask).count("1")


def _pick(allowed, k, avoid=0):
    bits = [b for b in range(allowed.bit_length()) if allowed >> b & 1]
    bits.sort(key=lambda b: (avoid >> b & 1, b))
    m = 0
    for b in bits[:k]:
        m |= 1 << b
    return m


def _plan(cores, topo):
    key = tuple(cores)
    if key in _CACHE:
        return _CACHE[key]
    n = len(cores)
    straight, hand = {}, {}
    for r in range(n):
        me = cores[r]
        near = [s for s in range(n) if s != r and topo.may_write(me, cores[s])]
        far = [s for s in range(n) if s != r and not topo.may_write(me, cores[s])]
        group = sorted(near + [r])
        i = group.index(r)
        straight[r] = group[i + 1:] + group[:i]
        owners = [h for h in range(max(cores) + topo.CORES_PER_CHIP)
                  if h not in cores and topo.host(h) == topo.host(me) and topo.chip(h) == topo.chip(me)
                  and all(topo.may_write(h, cores[s]) for s in far)]
        dies = sorted(set(topo.die(h) for h in owners), key=lambda d: (d != topo.die(me), d))
        free = {d: [h for h in owners if topo.die(h) == d] for d in dies}
        jobs = []
        for j, s in enumerate(far):
            turn = [dies[(i + j + t) % len(dies)] for t in range(len(dies))]
            d = [d for d in turn if free[d]][0]
            jobs.append((free[d].pop(0), s))
        rot = i % len(jobs) if jobs else 0
        hand[r] = jobs[rot:] + jobs[:rot]
    _CACHE[key] = (straight, hand)
    return _CACHE[key]


def _ids(topo, src, dsts):
    out = []
    for d in dsts:
        rid, pid = topo.addr(d, src)
        out.append(DstId(rid=rid, pnc=pid))
    return out


def _common(topo, src, dsts):
    m = topo.mask(src, dsts[0])
    for d in dsts:
        m &= topo.mask(src, d)
    return m


def _masks(cores, topo, r, straight, hand):
    me = cores[r]
    off = _common(topo, me, [cores[s] for s in straight[r]]) if straight[r] else 0
    m_straight = _pick(off, K_STRAIGHT)
    m_hand = _pick(_common(topo, me, [h for h, _ in hand[r]]), K_HAND, avoid=off) if hand[r] else 0
    return m_hand, m_straight


def rank_program(g, core, T, topo):
    cores = list(T.cores)
    n = len(cores)
    straight, hand = _plan(cores, topo)
    sem = T.sem

    def blk(lo, hi=None):
        return slice(lo * C, ((lo if hi is None else hi) + 1) * C)

    r = T.rank_of(core)
    if r is None:
        for o in range(n):
            mine = [s for h, s in hand[o] if h == core]
            if not mine:
                continue
            m_hand, _ = _masks(cores, topo, o, straight, hand)
            dsts = [cores[s] for s in mine]
            m = _pick(_common(topo, core, dsts), K_PASS)
            g.wait_ge(sem.hand, _count(m_hand))
            g.remote_dma_fused([RemoteDMATransfer(dst_ids=_ids(topo, core, dsts), dma_engine_mask=m,
                                                  remote_sem=sem["a%d" % o], srcs=[T.rl[:]],
                                                  dsts=[T.land[:, blk(o)] for _ in dsts], alu_op=0)], local_sem=sem.sent)
            g.wait_ge(sem.sent, _count(m))
        return

    g.sync.dma_start(T.xd[:], T.x[:]).then_inc(sem.ldd, 16)
    g.scalar.wait_ge(sem.ldd, 16)
    g.scalar.dma_start(T.land[:, blk(r)], T.x[:]).then_inc(sem.ldx, 16)

    m_hand, m_straight = _masks(cores, topo, r, straight, hand)
    g.wait_ge(sem.ldd, 16)
    if hand[r]:
        hs = [h for h, _ in hand[r]]
        g.remote_dma_fused([RemoteDMATransfer(dst_ids=_ids(topo, core, hs), dma_engine_mask=m_hand, remote_sem=sem.hand,
                                              srcs=[T.xd[:]], dsts=[T.rl[:] for _ in hs], alu_op=0)], local_sem=sem.sent)
    if straight[r]:
        ds = [cores[s] for s in straight[r]]
        g.remote_dma_fused([RemoteDMATransfer(dst_ids=_ids(topo, core, ds), dma_engine_mask=m_straight,
                                              remote_sem=sem["a%d" % r], srcs=[T.xd[:]],
                                              dsts=[T.land[:, blk(r)] for _ in ds], alu_op=0)], local_sem=sem.sent)
    g.wait_ge(sem.sent, _count(m_hand) + _count(m_straight))

    early = sorted((straight[s].index(r), s) for s in range(n) if r in straight[s])
    late = sorted(([d for _, d in hand[s]].index(r), s) for s in range(n) if r in [d for _, d in hand[s]])
    early, late = [s for _, s in early], [s for _, s in late]
    incs = {}
    for s in early:
        incs[s] = _count(_masks(cores, topo, s, straight, hand)[1])
    for s in late:
        h = [h for h, d in hand[s] if d == r][0]
        incs[s] = _count(_pick(_common(topo, h, [cores[d] for hh, d in hand[s] if hh == h]), K_PASS))

    last = list(range(min(late), max(late) + 1)) if late else []
    runs = []
    for s in range(n):
        if s in last:
            continue
        if runs and runs[-1][-1] == s - 1:
            runs[-1].append(s)
        else:
            runs.append([s])
    for run in runs:
        while run and run[0] == r:
            run.pop(0)
        while run and run[-1] == r:
            run.pop()
    runs = [run for run in runs if run] + ([last] if last else [])
    run_of = {s: i for i, run in enumerate(runs) for s in run}
    order = [s for s in [r] + early + late if s in run_of]

    g.tensor.wait_ge(sem.ldx, 16)
    for s in order:
        if s != r:
            g.tensor.wait_ge(sem["a%d" % s], incs[s])
        g.tensor.matmul(T["ps%d" % s][:, 0:C], T.land[:, blk(r)], T.land[:, blk(s)], True, True).then_inc(sem["m%d" % s], 1)
    for s in order:
        g.vector.wait_ge(sem["m%d" % s], 1)
        g.vector.tensor_copy(T.ysb[:, blk(s)], T["ps%d" % s][:, 0:C]).then_inc(sem["cp%d" % run_of[s]], 1)
    for i, run in enumerate(runs):
        q = g.scalar if run is runs[-1] else g.sync
        q.wait_ge(sem["cp%d" % i], len(run))
        q.dma_start(T.y[:, blk(run[0], run[-1])], T.ysb[:, blk(run[0], run[-1])]).then_inc(sem["st%d" % i], 16)
        q.wait_ge(sem["st%d" % i], 16)
